import numpy as np
import ml_dtypes


def mxq(x, axis, fmt="e4m3"):
    dtype, down = {"e4m3": (ml_dtypes.float8_e4m3fn, 7), "e5m2": (ml_dtypes.float8_e5m2, 14)}[fmt]
    v = np.moveaxis(np.asarray(x, np.float32).astype(ml_dtypes.bfloat16).astype(np.float64), axis, -1)
    blocks = v.reshape(v.shape[:-1] + (-1, 32))
    amax = np.abs(blocks).max(-1, keepdims=True)
    byte = np.maximum(np.where(amax > 0, np.frexp(amax)[1] - 1 + 127, 0) - down, 1)
    scale = np.exp2(byte - 127.0)
    codes = (blocks / scale).astype(np.float32).astype(dtype).astype(np.float64)
    return np.moveaxis((codes * scale).reshape(v.shape), -1, axis)


WIDE = False


def mx_kscale(k):
    if not WIDE:
        return np.ones(k)
    levels = np.array([10, -10, 5, -5, 0])
    if k % 512:
        return np.exp2(np.random.permutation(np.resize(levels, k // 32))).repeat(32)
    a = np.empty((k // 512, 16))
    for p in range(k // 512):
        a[p, :8] = np.random.permutation(np.resize(levels, 8))
        for g in range(8):
            far = levels[np.abs(levels - a[p, g]) >= 10]
            a[p, g + 8] = far[np.random.randint(len(far))]
    return np.exp2(a.ravel()).repeat(32)


def f64(x):
    return np.asarray(x).astype(np.float64)


def striped(idx):
    return np.tile(idx.reshape(-1, 16).T, (8, 1)).astype(np.uint16)


def unstriped(offs):
    return offs[:16].T.reshape(-1).astype(np.int64)


def pack_weight(w):
    k, n = w.shape
    w = f64(np.asarray(w, np.float32).astype(ml_dtypes.bfloat16)).reshape(k // 32, 32, n)
    amax = np.abs(w).max(1)
    byte = np.clip(np.where(amax > 0, np.frexp(amax)[1] - 1 + 127 - 7, 1), 1, 254)
    scaled = (w * np.exp2(127.0 - byte)[:, None, :]).reshape(k, n).astype(np.float32)
    words = np.ascontiguousarray(scaled.reshape(k // 512, 128, 4, n).transpose(0, 1, 3, 2)).astype(ml_dtypes.float8_e4m3fn).view(np.uint8)
    return words, np.ascontiguousarray(byte.astype(np.uint8).reshape(k // 512, 16, n))


def unpack_weight(words, scales):
    g, p, n, _ = words.shape
    vals = np.ascontiguousarray(words).view(ml_dtypes.float8_e4m3fn).astype(np.float64) * np.repeat(np.exp2(scales.astype(np.float64) - 127.0), 8, axis=1)[..., None]
    return vals.transpose(0, 1, 3, 2).reshape(g * 512, n)


K, T, S, G, W = 1024, 1024, 512, 512, 2048
P = 2 ** 7


def setup_inputs():
    n = np.random.standard_normal
    s = mx_kscale(K)[:, None]
    packed_xT = pack_weight(n((K, T)) * s)
    packed_eT = pack_weight(n((K, W)) * s)
    return {
        "x_words": packed_xT[0],
        "x_scales": packed_xT[1],
        "e_words": packed_eT[0],
        "e_scales": packed_eT[1],
        "ws": (n((K, G)) / np.sqrt(K) / s).astype(np.float32),
        "wt": (n((K, G)) / np.sqrt(K) / s).astype(np.float32),
        "cen": (np.tile(0.3 * n(G), (P, 1))).astype(np.float32),
        "offs": striped(np.random.permutation(T)[:S]),
        "tch": striped(np.random.permutation(W)[:S]),
    }


def reference(x_words, x_scales, e_words, e_scales, ws, wt, cen, offs, tch):
    xq = unpack_weight(x_words, x_scales)[:, unstriped(offs)]
    wsq = mxq(f64(ws), 0, "e4m3")
    y = 1.5 * (xq.T @ wsq)
    ex = np.exp(y - y.max(axis=1, keepdims=True))
    e_tch = unpack_weight(e_words, e_scales)[:, unstriped(tch)]
    wtq = mxq(f64(wt), 0, "e4m3")
    z = 2.5 * ((e_tch.T @ wtq) - f64(cen)[:1])
    ex2 = np.exp(z - z.max(axis=1, keepdims=True))
    p = ex2 / ex2.sum(axis=1, keepdims=True)
    return ex / ex.sum(axis=1, keepdims=True) - p

@@ -1,0 +1,165 @@
+from contextlib import ExitStack
+
+import concourse.mybir as mybir
+
+K, T, S, G, W = 1024, 1024, 512, 512, 2048
+FLOPS = 2 * 2 * K * S * G
+
+F32 = mybir.dt.float32
+BF16 = mybir.dt.bfloat16
+I32 = mybir.dt.int32
+U32 = mybir.dt.uint32
+U16 = mybir.dt.uint16
+U8 = mybir.dt.uint8
+FP8X4 = mybir.dt.float8_e4m3fn_x4
+ALU = mybir.AluOpType
+ACT = mybir.ActivationFunctionType
+
+P = 128
+PACK = 4
+K_PASS = P * PACK
+PASSES = K // K_PASS
+TILES = S // P
+PER_COL = 16
+HALF = G // 2
+
+
+def tile_picked_ydino_grad_p_kernel(
+    tc, x_words, x_scales, e_words, e_scales, ws, wt, cen, offs, tch, out
+):
+    nc = tc.nc
+    with ExitStack() as ctx:
+        keep = ctx.enter_context(tc.tile_pool(name="keep", bufs=1))
+        psum = ctx.enter_context(tc.psum_pool(name="psum", bufs=1))
+
+        def load_list(name, src):
+            tile = keep.tile([P, S // PER_COL], U16, name=name)
+            nc.sync.dma_start(tile[:], src)
+            return tile
+
+        def load_scale_rows(name, src, width, clear, queue):
+            tile = keep.tile([P, width], U8, name=name, align_bytes=64)
+            clear.memset(tile[:].bitcast(I32), 0)
+            for q in range(4):
+                queue.dma_start(
+                    tile[32 * q : 32 * q + 4 * PASSES, :].bitcast(I32),
+                    src[:, 4 * q : 4 * q + 4, :].bitcast(I32),
+                )
+            return tile
+
+        def load_words(name, src, o, width):
+            tile = keep.tile([P, width], U32, name=name, align_bytes=64)
+            nc.sync.dma_start(tile[:].bitcast(I32), src[o].rearrange("p n t -> p (n t)").bitcast(I32))
+            return tile
+
+        def load_weight(name, src, o):
+            tile = keep.tile([P, PACK, G], F32, name=name)
+            rows = src[o * K_PASS : (o + 1) * K_PASS, :]
+            nc.sync.dma_start(tile[:], rows.rearrange("(p j) g -> p j g", j=PACK))
+            return tile
+
+        def quantise(name, raw):
+            codes = keep.tile([P, G], U32, name=name + "_codes", align_bytes=64)
+            scales = keep.tile([P, G], U8, name=name + "_scales", align_bytes=64)
+            for h in range(2):
+                cols = slice(h * HALF, (h + 1) * HALF)
+                grouped = keep.tile([P, HALF, PACK], BF16, name=name + "_bf%d" % h, align_bytes=64)
+                nc.scalar.copy(
+                    grouped[:].rearrange("p (c i) t -> p c t i", i=4),
+                    raw[:, :, cols].rearrange("p t (c i) -> p c t i", i=4),
+                )
+                nc.vector.quantize_mx(
+                    out=codes[:, cols].bitcast(FP8X4),
+                    scales=scales[:, cols],
+                    in_=grouped[:].rearrange("p c t -> p (c t)"),
+                )
+            return codes, scales
+
+        def gather(name, table, lst, dtype, first, count):
+            tile = keep.tile([P, count], dtype, name=name, align_bytes=64)
+            nc.vector.tensor_copy(
+                tile[:], table[:].indirect(lst[:, first // PER_COL : (first + count) // PER_COL])
+            )
+            return tile
+
+        def mx_pass(acc, o, words, word_cols, picked_scales, t, weight):
+            nc.tensor.matmul_mx(
+                out=acc[:],
+                lhsT=words[:, word_cols].bitcast(FP8X4),
+                lhsT_scale=picked_scales[4 * o :, t * P : (t + 1) * P],
+                rhs=weight[0][:].bitcast(FP8X4),
+                rhs_scale=weight[1][:],
+                start=(o == 0),
+                stop=(o == PASSES - 1),
+            )
+
+        e_rows = load_scale_rows("e_rows", e_scales, W, nc.vector, nc.scalar)
+        wt_raw = [load_weight("wt_raw0", wt, 0)]
+        tch_list = load_list("tch_list", tch)
+        wt_raw.append(load_weight("wt_raw1", wt, 1))
+        offs_list = load_list("offs_list", offs)
+        x_rows = load_scale_rows("x_rows", x_scales, T, nc.gpsimd, nc.sync)
+        e_tab = [load_words("e_tab%d" % o, e_words, o, W) for o in range(PASSES)]
+        cen_sb = keep.tile([P, G], F32, name="cen_sb")
+        nc.sync.dma_start(cen_sb[:], cen)
+        ws_raw = [load_weight("ws_raw%d" % o, ws, o) for o in range(PASSES)]
+        x_tab = [load_words("x_tab%d" % o, x_words, o, T) for o in range(PASSES)]
+
+        e_sc = gather("e_sc", e_rows, tch_list, U8, 0, S)
+        wt_q = [quantise("wt0", wt_raw[0])]
+        x_sc = gather("x_sc", x_rows, offs_list, U8, 0, S)
+        wt_q.append(quantise("wt1", wt_raw[1]))
+        e0 = gather("e0", e_tab[0], tch_list, U32, 0, S)
+        acc_t = [psum.tile([P, G], F32, name="acc_t%d" % t) for t in range(TILES)]
+        for t in range(TILES):
+            mx_pass(acc_t[t], 0, e0, slice(t * P, (t + 1) * P), e_sc, t, wt_q[0])
+        prob = []
+        t_exp = []
+        t_sum = []
+        ws_q = []
+        for t in range(TILES):
+            if t % 2 == 0:
+                e1 = gather("e1_%d" % t, e_tab[1], tch_list, U32, t * P, 2 * P)
+            mx_pass(acc_t[t], 1, e1, slice((t % 2) * P, (t % 2 + 1) * P), e_sc, t, wt_q[1])
+            neg = keep.tile([P, G], F32, name="t_neg%d" % t)
+            low = keep.tile([P, 1], F32, name="t_low%d" % t)
+            nc.vector.tensor_tensor(neg[:], cen_sb[:], acc_t[t][:], ALU.subtract)
+            nc.vector.tensor_scalar(neg[:], neg[:], 2.5, None, ALU.mult, ALU.min, accum_out=low[:])
+            ex = keep.tile([P, G], F32, name="t_exp%d" % t)
+            total = keep.tile([P, 1], F32, name="t_sum%d" % t)
+            nc.scalar.activation(ex[:], neg[:], ACT.Exp, bias=low[:], scale=-1.0, accum_out=total[:])
+            t_exp.append(ex)
+            t_sum.append(total)
+        for o in range(PASSES):
+            ws_q.append(quantise("ws%d" % o, ws_raw[o]))
+        x0 = gather("x0", x_tab[0], offs_list, U32, 0, S)
+        for t in range(TILES):
+            inv = keep.tile([P, 1], F32, name="t_inv%d" % t)
+            nc.vector.reciprocal(inv[:], t_sum[t][:])
+            p_t = keep.tile([P, G], F32, name="prob%d" % t)
+            nc.scalar.activation(p_t[:], t_exp[t][:], ACT.Copy, scale=inv[:])
+            prob.append(p_t)
+
+        acc_s = [psum.tile([P, G], F32, name="acc_s%d" % t) for t in range(TILES)]
+        for t in range(TILES):
+            mx_pass(acc_s[t], 0, x0, slice(t * P, (t + 1) * P), x_sc, t, ws_q[0])
+        s_exp = []
+        s_sum = []
+        for t in range(TILES):
+            x1 = gather("x1_%d" % t, x_tab[1], offs_list, U32, t * P, P)
+            mx_pass(acc_s[t], 1, x1, slice(0, P), x_sc, t, ws_q[1])
+        for t in range(TILES):
+            neg = keep.tile([P, G], F32, name="s_neg%d" % t)
+            low = keep.tile([P, 1], F32, name="s_low%d" % t)
+            nc.vector.tensor_scalar(neg[:], acc_s[t][:], -1.5, None, ALU.mult, ALU.min, accum_out=low[:])
+            ex = keep.tile([P, G], F32, name="s_exp%d" % t)
+            total = keep.tile([P, 1], F32, name="s_sum%d" % t)
+            nc.scalar.activation(ex[:], neg[:], ACT.Exp, bias=low[:], scale=-1.0, accum_out=total[:])
+            s_exp.append(ex)
+            s_sum.append(total)
+        for t in range(TILES):
+            inv = keep.tile([P, 1], F32, name="s_inv%d" % t)
+            nc.vector.reciprocal(inv[:], s_sum[t][:])
+            res = keep.tile([P, G], F32, name="res%d" % t)
+            nc.vector.scalar_tensor_tensor(res[:], s_exp[t][:], inv[:], prob[t][:], ALU.mult, ALU.subtract)
+            nc.sync.dma_start(out[t * P : (t + 1) * P, :], res[:])

@@ -37,11 +37,11 @@ def tile_picked_ydino_grad_p_kernel(
             nc.sync.dma_start(tile[:], src)
             return tile
 
-        def load_scale_rows(name, src, width, clear, queue):
+        def load_scale_rows(name, src, width):
             tile = keep.tile([P, width], U8, name=name, align_bytes=64)
-            clear.memset(tile[:].bitcast(I32), 0)
+            nc.vector.memset(tile[:].bitcast(I32), 0)
             for q in range(4):
-                queue.dma_start(
+                nc.gpsimd.dma_start(
                     tile[32 * q : 32 * q + 4 * PASSES, :].bitcast(I32),
                     src[:, 4 * q : 4 * q + 4, :].bitcast(I32),
                 )
@@ -58,22 +58,26 @@ def tile_picked_ydino_grad_p_kernel(
             nc.sync.dma_start(tile[:], rows.rearrange("(p j) g -> p j g", j=PACK))
             return tile
 
-        def quantise(name, raw):
-            codes = keep.tile([P, G], U32, name=name + "_codes", align_bytes=64)
-            scales = keep.tile([P, G], U8, name=name + "_scales", align_bytes=64)
+        def round_and_group(name, raw, copies):
+            grouped = keep.tile([P, G, PACK], BF16, name=name + "_bf", align_bytes=64)
             for h in range(2):
                 cols = slice(h * HALF, (h + 1) * HALF)
-                grouped = keep.tile([P, HALF, PACK], BF16, name=name + "_bf%d" % h, align_bytes=64)
-                nc.scalar.copy(
-                    grouped[:].rearrange("p (c i) t -> p c t i", i=4),
+                copies[h](
+                    grouped[:, cols, :].rearrange("p (c i) t -> p c t i", i=4),
                     raw[:, :, cols].rearrange("p t (c i) -> p c t i", i=4),
                 )
-                nc.vector.quantize_mx(
-                    out=codes[:, cols].bitcast(FP8X4),
-                    scales=scales[:, cols],
-                    in_=grouped[:].rearrange("p c t -> p (c t)"),
-                )
+            return grouped
+
+        def quantise(name, grouped):
+            codes = keep.tile([P, G], U32, name=name + "_codes", align_bytes=64)
+            scales = keep.tile([P, G], U8, name=name + "_scales", align_bytes=64)
+            nc.vector.quantize_mx(
+                out=codes[:].bitcast(FP8X4),
+                scales=scales[:],
+                in_=grouped[:].rearrange("p c t -> p (c t)"),
+            )
             return codes, scales
+
 
         def gather(name, table, lst, dtype, first, count):
             tile = keep.tile([P, count], dtype, name=name, align_bytes=64)
@@ -93,61 +97,67 @@ def tile_picked_ydino_grad_p_kernel(
                 stop=(o == PASSES - 1),
             )
 
-        e_rows = load_scale_rows("e_rows", e_scales, W, nc.vector, nc.scalar)
+        e_rows = load_scale_rows("e_rows", e_scales, W)
+        x_rows = load_scale_rows("x_rows", x_scales, T)
         wt_raw = [load_weight("wt_raw0", wt, 0)]
         tch_list = load_list("tch_list", tch)
-        wt_raw.append(load_weight("wt_raw1", wt, 1))
         offs_list = load_list("offs_list", offs)
-        x_rows = load_scale_rows("x_rows", x_scales, T, nc.gpsimd, nc.sync)
-        e_tab = [load_words("e_tab%d" % o, e_words, o, W) for o in range(PASSES)]
+        e_tab = [load_words("e_tab0", e_words, 0, W)]
+        wt_raw.append(load_weight("wt_raw1", wt, 1))
+        e_tab.append(load_words("e_tab1", e_words, 1, W))
         cen_sb = keep.tile([P, G], F32, name="cen_sb")
         nc.sync.dma_start(cen_sb[:], cen)
         ws_raw = [load_weight("ws_raw%d" % o, ws, o) for o in range(PASSES)]
         x_tab = [load_words("x_tab%d" % o, x_words, o, T) for o in range(PASSES)]
 
+        on_scalar = (nc.scalar.copy, nc.scalar.copy)
+        wt_bf = [round_and_group("wt0", wt_raw[0], on_scalar)]
+        ws_bf = [round_and_group("ws%d" % o, ws_raw[o], on_scalar) for o in range(PASSES)]
+
         e_sc = gather("e_sc", e_rows, tch_list, U8, 0, S)
-        wt_q = [quantise("wt0", wt_raw[0])]
-        x_sc = gather("x_sc", x_rows, offs_list, U8, 0, S)
-        wt_q.append(quantise("wt1", wt_raw[1]))
-        e0 = gather("e0", e_tab[0], tch_list, U32, 0, S)
+        wt_q = [quantise("wt0", wt_bf[0])]
         acc_t = [psum.tile([P, G], F32, name="acc_t%d" % t) for t in range(TILES)]
-        for t in range(TILES):
-            mx_pass(acc_t[t], 0, e0, slice(t * P, (t + 1) * P), e_sc, t, wt_q[0])
-        prob = []
-        t_exp = []
-        t_sum = []
-        ws_q = []
-        for t in range(TILES):
-            if t % 2 == 0:
-                e1 = gather("e1_%d" % t, e_tab[1], tch_list, U32, t * P, 2 * P)
-            mx_pass(acc_t[t], 1, e1, slice((t % 2) * P, (t % 2 + 1) * P), e_sc, t, wt_q[1])
-            neg = keep.tile([P, G], F32, name="t_neg%d" % t)
-            low = keep.tile([P, 1], F32, name="t_low%d" % t)
-            nc.vector.tensor_tensor(neg[:], cen_sb[:], acc_t[t][:], ALU.subtract)
-            nc.vector.tensor_scalar(neg[:], neg[:], 2.5, None, ALU.mult, ALU.min, accum_out=low[:])
-            ex = keep.tile([P, G], F32, name="t_exp%d" % t)
-            total = keep.tile([P, 1], F32, name="t_sum%d" % t)
-            nc.scalar.activation(ex[:], neg[:], ACT.Exp, bias=low[:], scale=-1.0, accum_out=total[:])
-            t_exp.append(ex)
-            t_sum.append(total)
         for o in range(PASSES):
-            ws_q.append(quantise("ws%d" % o, ws_raw[o]))
-        x0 = gather("x0", x_tab[0], offs_list, U32, 0, S)
-        for t in range(TILES):
-            inv = keep.tile([P, 1], F32, name="t_inv%d" % t)
-            nc.vector.reciprocal(inv[:], t_sum[t][:])
-            p_t = keep.tile([P, G], F32, name="prob%d" % t)
-            nc.scalar.activation(p_t[:], t_exp[t][:], ACT.Copy, scale=inv[:])
-            prob.append(p_t)
+            if o == 1:
+                shared = round_and_group("wt1", wt_raw[1], (nc.scalar.copy, nc.vector.tensor_copy))
+                wt_q.append(quantise("wt1", shared))
+                x_sc = gather("x_sc", x_rows, offs_list, U8, 0, S)
+            for t in range(TILES):
+                if t % 2 == 0:
+                    picked = gather("e%d_%d" % (o, t), e_tab[o], tch_list, U32, t * P, 2 * P)
+                mx_pass(acc_t[t], o, picked, slice((t % 2) * P, (t % 2 + 1) * P), e_sc, t, wt_q[o])
 
         acc_s = [psum.tile([P, G], F32, name="acc_s%d" % t) for t in range(TILES)]
+        ws_q = [quantise("ws0", ws_bf[0])]
         for t in range(TILES):
-            mx_pass(acc_s[t], 0, x0, slice(t * P, (t + 1) * P), x_sc, t, ws_q[0])
-        s_exp = []
-        s_sum = []
+            if t % 2 == 0:
+                x0 = gather("x0_%d" % t, x_tab[0], offs_list, U32, t * P, 2 * P)
+            mx_pass(acc_s[t], 0, x0, slice((t % 2) * P, (t % 2 + 1) * P), x_sc, t, ws_q[0])
+        ws_q.append(quantise("ws1", ws_bf[1]))
         for t in range(TILES):
             x1 = gather("x1_%d" % t, x_tab[1], offs_list, U32, t * P, P)
             mx_pass(acc_s[t], 1, x1, slice(0, P), x_sc, t, ws_q[1])
+
+        t_neg = [keep.tile([P, G], F32, name="t_neg%d" % t) for t in range(TILES)]
+        t_exp = [ws_raw[1][:, t, :] for t in range(TILES)]
+        t_low = [keep.tile([P, 1], F32, name="t_low%d" % t) for t in range(TILES)]
+        t_sum = keep.tile([P, TILES], F32, name="t_sum")
+        for step in range(TILES + 1):
+            if step < TILES:
+                nc.vector.tensor_tensor(t_neg[step][:], cen_sb[:], acc_t[step][:], ALU.subtract)
+            if step > 0:
+                t = step - 1
+                nc.vector.tensor_scalar(
+                    t_neg[t][:], t_neg[t][:], 2.5, None, ALU.mult, ALU.min, accum_out=t_low[t][:]
+                )
+                nc.scalar.activation(
+                    t_exp[t], t_neg[t][:], ACT.Exp, bias=t_low[t][:], scale=-1.0, accum_out=t_sum[:, t : t + 1]
+                )
+
+        t_inv = keep.tile([P, TILES], F32, name="t_inv")
+        nc.vector.reciprocal(t_inv[:], t_sum[:])
+        s_exp = []
+        s_sum = []
         for t in range(TILES):
             neg = keep.tile([P, G], F32, name="s_neg%d" % t)
             low = keep.tile([P, 1], F32, name="s_low%d" % t)
@@ -157,9 +167,12 @@ def tile_picked_ydino_grad_p_kernel(
             nc.scalar.activation(ex[:], neg[:], ACT.Exp, bias=low[:], scale=-1.0, accum_out=total[:])
             s_exp.append(ex)
             s_sum.append(total)
+
         for t in range(TILES):
+            p_t = keep.tile([P, G], F32, name="prob%d" % t)
+            nc.gpsimd.tensor_scalar(p_t[:], t_exp[t], t_inv[:, t : t + 1], 0.0, ALU.mult, ALU.add)
             inv = keep.tile([P, 1], F32, name="s_inv%d" % t)
             nc.vector.reciprocal(inv[:], s_sum[t][:])
             res = keep.tile([P, G], F32, name="res%d" % t)
-            nc.vector.scalar_tensor_tensor(res[:], s_exp[t][:], inv[:], prob[t][:], ALU.mult, ALU.subtract)
+            nc.vector.scalar_tensor_tensor(res[:], s_exp[t][:], inv[:], p_t[:], ALU.mult, ALU.subtract)
             nc.sync.dma_start(out[t * P : (t + 1) * P, :], res[:])

@@ -14,6 +14,7 @@ U8 = mybir.dt.uint8
 FP8X4 = mybir.dt.float8_e4m3fn_x4
 ALU = mybir.AluOpType
 ACT = mybir.ActivationFunctionType
+AX = mybir.AxisListType
 
 P = 128
 PACK = 4
@@ -38,13 +39,20 @@ def tile_picked_ydino_grad_p_kernel(
             return tile
 
         def load_scale_rows(name, src, width):
+            stage = keep.tile([P, width], U8, name=name + "_stage", align_bytes=64)
+            for q in range(4):
+                nc.sync.dma_start(
+                    stage[32 * q : 32 * q + 4 * PASSES, :].bitcast(I32),
+                    src[:, 4 * q : 4 * q + 4, :].bitcast(I32),
+                )
+            return stage
+
+        def place_scale_rows(name, stage, width):
             tile = keep.tile([P, width], U8, name=name, align_bytes=64)
             nc.vector.memset(tile[:].bitcast(I32), 0)
             for q in range(4):
-                nc.gpsimd.dma_start(
-                    tile[32 * q : 32 * q + 4 * PASSES, :].bitcast(I32),
-                    src[:, 4 * q : 4 * q + 4, :].bitcast(I32),
-                )
+                rows = slice(32 * q, 32 * q + 4 * PASSES)
+                nc.vector.tensor_copy(tile[rows, :].bitcast(I32), stage[rows, :].bitcast(I32))
             return tile
 
         def load_words(name, src, o, width):
@@ -97,10 +105,10 @@ def tile_picked_ydino_grad_p_kernel(
                 stop=(o == PASSES - 1),
             )
 
-        e_rows = load_scale_rows("e_rows", e_scales, W)
-        x_rows = load_scale_rows("x_rows", x_scales, T)
-        wt_raw = [load_weight("wt_raw0", wt, 0)]
         tch_list = load_list("tch_list", tch)
+        e_stage = load_scale_rows("e_rows", e_scales, W)
+        wt_raw = [load_weight("wt_raw0", wt, 0)]
+        x_stage = load_scale_rows("x_rows", x_scales, T)
         offs_list = load_list("offs_list", offs)
         e_tab = [load_words("e_tab0", e_words, 0, W)]
         wt_raw.append(load_weight("wt_raw1", wt, 1))
@@ -114,14 +122,16 @@ def tile_picked_ydino_grad_p_kernel(
         wt_bf = [round_and_group("wt0", wt_raw[0], on_scalar)]
         ws_bf = [round_and_group("ws%d" % o, ws_raw[o], on_scalar) for o in range(PASSES)]
 
+        e_rows = place_scale_rows("e_rows", e_stage, W)
         e_sc = gather("e_sc", e_rows, tch_list, U8, 0, S)
+        x_rows = place_scale_rows("x_rows", x_stage, T)
+        x_sc = gather("x_sc", x_rows, offs_list, U8, 0, S)
         wt_q = [quantise("wt0", wt_bf[0])]
         acc_t = [psum.tile([P, G], F32, name="acc_t%d" % t) for t in range(TILES)]
         for o in range(PASSES):
             if o == 1:
                 shared = round_and_group("wt1", wt_raw[1], (nc.scalar.copy, nc.vector.tensor_copy))
                 wt_q.append(quantise("wt1", shared))
-                x_sc = gather("x_sc", x_rows, offs_list, U8, 0, S)
             for t in range(TILES):
                 if t % 2 == 0:
                     picked = gather("e%d_%d" % (o, t), e_tab[o], tch_list, U32, t * P, 2 * P)
@@ -138,39 +148,42 @@ def tile_picked_ydino_grad_p_kernel(
             x1 = gather("x1_%d" % t, x_tab[1], offs_list, U32, t * P, P)
             mx_pass(acc_s[t], 1, x1, slice(0, P), x_sc, t, ws_q[1])
 
-        t_neg = [keep.tile([P, G], F32, name="t_neg%d" % t) for t in range(TILES)]
-        t_exp = [ws_raw[1][:, t, :] for t in range(TILES)]
-        t_low = [keep.tile([P, 1], F32, name="t_low%d" % t) for t in range(TILES)]
-        t_sum = keep.tile([P, TILES], F32, name="t_sum")
-        for step in range(TILES + 1):
-            if step < TILES:
-                nc.vector.tensor_tensor(t_neg[step][:], cen_sb[:], acc_t[step][:], ALU.subtract)
-            if step > 0:
-                t = step - 1
-                nc.vector.tensor_scalar(
-                    t_neg[t][:], t_neg[t][:], 2.5, None, ALU.mult, ALU.min, accum_out=t_low[t][:]
-                )
+        t_exp = [ws_raw[t // 2][:, t % 2, :] for t in range(TILES)]
+        t_inv = []
+        for pair in range(TILES // 2):
+            neg = keep.tile([P, 2, G], F32, name="t_neg%d" % pair)
+            for u in range(2):
+                nc.vector.tensor_tensor(neg[:, u, :], cen_sb[:], acc_t[2 * pair + u][:], ALU.subtract)
+            low = keep.tile([P, 2], F32, name="t_low%d" % pair)
+            nc.vector.tensor_reduce(low[:], neg[:], AX.X, ALU.min)
+            shift = keep.tile([P, 2], F32, name="t_shift%d" % pair)
+            t_sum = keep.tile([P, 2], F32, name="t_sum%d" % pair)
+            nc.scalar.mul(shift[:], low[:], 2.5)
+            for u in range(2):
+                t = 2 * pair + u
                 nc.scalar.activation(
-                    t_exp[t], t_neg[t][:], ACT.Exp, bias=t_low[t][:], scale=-1.0, accum_out=t_sum[:, t : t + 1]
+                    t_exp[t], neg[:, u, :], ACT.Exp, bias=shift[:, u : u + 1], scale=-2.5, accum_out=t_sum[:, u : u + 1]
                 )
+            inv = keep.tile([P, 2], F32, name="t_inv%d" % pair)
+            nc.vector.reciprocal(inv[:], t_sum[:])
+            t_inv.extend([inv[:, 0:1], inv[:, 1:2]])
 
-        t_inv = keep.tile([P, TILES], F32, name="t_inv")
-        nc.vector.reciprocal(t_inv[:], t_sum[:])
         s_exp = []
         s_sum = []
         for t in range(TILES):
-            neg = keep.tile([P, G], F32, name="s_neg%d" % t)
-            low = keep.tile([P, 1], F32, name="s_low%d" % t)
-            nc.vector.tensor_scalar(neg[:], acc_s[t][:], -1.5, None, ALU.mult, ALU.min, accum_out=low[:])
+            top = keep.tile([P, 1], F32, name="s_top%d" % t)
+            nc.vector.tensor_reduce(top[:], acc_s[t][:], AX.X, ALU.max)
+            shift = keep.tile([P, 1], F32, name="s_shift%d" % t)
+            nc.scalar.mul(shift[:], top[:], -1.5)
             ex = keep.tile([P, G], F32, name="s_exp%d" % t)
             total = keep.tile([P, 1], F32, name="s_sum%d" % t)
-            nc.scalar.activation(ex[:], neg[:], ACT.Exp, bias=low[:], scale=-1.0, accum_out=total[:])
+            nc.scalar.activation(ex[:], acc_s[t][:], ACT.Exp, bias=shift[:], scale=1.5, accum_out=total[:])
             s_exp.append(ex)
             s_sum.append(total)
 
         for t in range(TILES):
             p_t = keep.tile([P, G], F32, name="prob%d" % t)
-            nc.gpsimd.tensor_scalar(p_t[:], t_exp[t], t_inv[:, t : t + 1], 0.0, ALU.mult, ALU.add)
+            nc.scalar.activation(p_t[:], t_exp[t], ACT.Copy, scale=t_inv[t])
             inv = keep.tile([P, 1], F32, name="s_inv%d" % t)
             nc.vector.reciprocal(inv[:], s_sum[t][:])
             res = keep.tile([P, G], F32, name="res%d" % t)

@@ -1,8 +1,15 @@
 from contextlib import ExitStack
 
 import concourse.mybir as mybir
+from concourse.masks import make_identity
 
-K, T, S, G, W = 1024, 1024, 512, 512, 2048
+K = 1024
+T = 1024
+W = 2048
+S = 512
+G = 512
+STUDENT_GAIN = 1.5
+TEACHER_GAIN = 2.5
 FLOPS = 2 * 2 * K * S * G
 
 F32 = mybir.dt.float32
@@ -21,39 +28,40 @@ PACK = 4
 K_PASS = P * PACK
 PASSES = K // K_PASS
 TILES = S // P
-PER_COL = 16
-HALF = G // 2
+QUADRANTS = 4
+SCALE_ROWS = 4
+LIST_COLS = S // 16
+LINE = 4
+
+assert S == G
 
 
 def tile_picked_ydino_grad_p_kernel(
     tc, x_words, x_scales, e_words, e_scales, ws, wt, cen, offs, tch, out
 ):
     nc = tc.nc
+    whole = slice(0, G)
+    halves = [slice(0, G // 2), slice(G // 2, G)]
+    blocks = [slice(j * P, (j + 1) * P) for j in range(TILES)]
+
     with ExitStack() as ctx:
         keep = ctx.enter_context(tc.tile_pool(name="keep", bufs=1))
         psum = ctx.enter_context(tc.psum_pool(name="psum", bufs=1))
 
         def load_list(name, src):
-            tile = keep.tile([P, S // PER_COL], U16, name=name)
+            tile = keep.tile([P, LIST_COLS], U16, name=name)
             nc.sync.dma_start(tile[:], src)
             return tile
 
-        def load_scale_rows(name, src, width):
-            stage = keep.tile([P, width], U8, name=name + "_stage", align_bytes=64)
-            for q in range(4):
-                nc.sync.dma_start(
-                    stage[32 * q : 32 * q + 4 * PASSES, :].bitcast(I32),
-                    src[:, 4 * q : 4 * q + 4, :].bitcast(I32),
-                )
-            return stage
+        def live_rows(q):
+            return slice(32 * q, 32 * q + SCALE_ROWS * PASSES)
 
-        def place_scale_rows(name, stage, width):
-            tile = keep.tile([P, width], U8, name=name, align_bytes=64)
-            nc.vector.memset(tile[:].bitcast(I32), 0)
-            for q in range(4):
-                rows = slice(32 * q, 32 * q + 4 * PASSES)
-                nc.vector.tensor_copy(tile[rows, :].bitcast(I32), stage[rows, :].bitcast(I32))
-            return tile
+        def load_scale_rows(tile, src):
+            for q in range(QUADRANTS):
+                nc.sync.dma_start(
+                    tile[live_rows(q), :].bitcast(I32),
+                    src[:, SCALE_ROWS * q : SCALE_ROWS * (q + 1), :].bitcast(I32),
+                )
 
         def load_words(name, src, o, width):
             tile = keep.tile([P, width], U32, name=name, align_bytes=64)
@@ -66,107 +74,144 @@ def tile_picked_ydino_grad_p_kernel(
             nc.sync.dma_start(tile[:], rows.rearrange("(p j) g -> p j g", j=PACK))
             return tile
 
-        def round_and_group(name, raw, copies):
+        def weight_tiles(name):
             grouped = keep.tile([P, G, PACK], BF16, name=name + "_bf", align_bytes=64)
-            for h in range(2):
-                cols = slice(h * HALF, (h + 1) * HALF)
-                copies[h](
-                    grouped[:, cols, :].rearrange("p (c i) t -> p c t i", i=4),
-                    raw[:, :, cols].rearrange("p t (c i) -> p c t i", i=4),
-                )
-            return grouped
-
-        def quantise(name, grouped):
             codes = keep.tile([P, G], U32, name=name + "_codes", align_bytes=64)
             scales = keep.tile([P, G], U8, name=name + "_scales", align_bytes=64)
+            return grouped, (codes, scales)
+
+        def round_and_group(copy, grouped, raw, cols):
+            copy(
+                grouped[:, cols, :].rearrange("p (c i) j -> p c j i", i=LINE),
+                raw[:, :, cols].rearrange("p j (c i) -> p c j i", i=LINE),
+            )
+
+        def quantise(weight, grouped, cols):
             nc.vector.quantize_mx(
-                out=codes[:].bitcast(FP8X4),
-                scales=scales[:],
-                in_=grouped[:].rearrange("p c t -> p (c t)"),
+                out=weight[0][:, cols].bitcast(FP8X4),
+                scales=weight[1][:, cols],
+                in_=grouped[:, cols, :].rearrange("p c j -> p (c j)"),
             )
-            return codes, scales
 
-
-        def gather(name, table, lst, dtype, first, count):
-            tile = keep.tile([P, count], dtype, name=name, align_bytes=64)
-            nc.vector.tensor_copy(
-                tile[:], table[:].indirect(lst[:, first // PER_COL : (first + count) // PER_COL])
-            )
+        def gather(name, table, entries, dtype):
+            tile = keep.tile([P, S], dtype, name=name, align_bytes=64)
+            nc.vector.tensor_copy(tile[:], table[:].indirect(entries[:]))
             return tile
 
-        def mx_pass(acc, o, words, word_cols, picked_scales, t, weight):
+        x_rows = keep.tile([P, T], U8, name="x_rows", align_bytes=64)
+        nc.gpsimd.memset(x_rows[:].bitcast(I32), 0)
+        e_stage = keep.tile([P, W], U8, name="e_stage", align_bytes=64)
+        tch_list = load_list("tch_list", tch)
+        load_scale_rows(e_stage, e_scales)
+        wt_raw = [load_weight("wt_raw0", wt, 0)]
+        load_scale_rows(x_rows, x_scales)
+        offs_list = load_list("offs_list", offs)
+        cen_rows = keep.tile([P, P], F32, name="cen_rows")
+        nc.gpsimd.memset(cen_rows[:], 0.0)
+        nc.sync.dma_start(cen_rows[0:TILES, :], cen[0].rearrange("(j p) -> j p", p=P))
+        e_tab = [load_words("e_tab%d" % o, e_words, o, W) for o in range(PASSES)]
+        wt_raw.append(load_weight("wt_raw1", wt, 1))
+        x_tab = [load_words("x_tab%d" % o, x_words, o, T) for o in range(PASSES)]
+        ws_raw = [load_weight("ws_raw%d" % o, ws, o) for o in range(PASSES)]
+
+        ident = keep.tile([P, P], F32, name="ident")
+        make_identity(nc, ident[:])
+
+        neg_z = [psum.tile([P, G], F32, name="neg_z%d" % t, tag="neg_z%d" % t) for t in range(TILES)]
+        nc.tensor.transpose(neg_z[0][:, 0:P], cen_rows[:], ident[:])
+        cen_col = keep.tile([P, TILES], F32, name="cen_col")
+        nc.scalar.mul(cen_col[:], neg_z[0][:, 0:TILES], TEACHER_GAIN)
+
+        e_rows = keep.tile([P, W], U8, name="e_rows", align_bytes=64)
+        nc.gpsimd.memset(e_rows[:].bitcast(I32), 0)
+        for q in range(QUADRANTS):
+            nc.vector.tensor_copy(e_rows[live_rows(q), :].bitcast(I32), e_stage[live_rows(q), :].bitcast(I32))
+        e_sc = gather("e_sc", e_rows, tch_list, U8)
+        x_sc = gather("x_sc", x_rows, offs_list, U8)
+
+        acc_t = [psum.tile([P, S], F32, name="acc_t%d" % j, tag="acc%d" % j) for j in range(TILES)]
+
+        def teacher_pass(o, j, weight, picked):
             nc.tensor.matmul_mx(
-                out=acc[:],
-                lhsT=words[:, word_cols].bitcast(FP8X4),
-                lhsT_scale=picked_scales[4 * o :, t * P : (t + 1) * P],
-                rhs=weight[0][:].bitcast(FP8X4),
-                rhs_scale=weight[1][:],
+                out=acc_t[j][:],
+                lhsT=weight[0][:, blocks[j]].bitcast(FP8X4),
+                lhsT_scale=weight[1][:, blocks[j]],
+                rhs=picked[:].bitcast(FP8X4),
+                rhs_scale=e_sc[SCALE_ROWS * o :, :],
                 start=(o == 0),
                 stop=(o == PASSES - 1),
             )
 
-        tch_list = load_list("tch_list", tch)
-        e_stage = load_scale_rows("e_rows", e_scales, W)
-        wt_raw = [load_weight("wt_raw0", wt, 0)]
-        x_stage = load_scale_rows("x_rows", x_scales, T)
-        offs_list = load_list("offs_list", offs)
-        e_tab = [load_words("e_tab0", e_words, 0, W)]
-        wt_raw.append(load_weight("wt_raw1", wt, 1))
-        e_tab.append(load_words("e_tab1", e_words, 1, W))
-        cen_sb = keep.tile([P, G], F32, name="cen_sb")
-        nc.sync.dma_start(cen_sb[:], cen)
-        ws_raw = [load_weight("ws_raw%d" % o, ws, o) for o in range(PASSES)]
-        x_tab = [load_words("x_tab%d" % o, x_words, o, T) for o in range(PASSES)]
-
-        on_scalar = (nc.scalar.copy, nc.scalar.copy)
-        wt_bf = [round_and_group("wt0", wt_raw[0], on_scalar)]
-        ws_bf = [round_and_group("ws%d" % o, ws_raw[o], on_scalar) for o in range(PASSES)]
-
-        e_rows = place_scale_rows("e_rows", e_stage, W)
-        e_sc = gather("e_sc", e_rows, tch_list, U8, 0, S)
-        x_rows = place_scale_rows("x_rows", x_stage, T)
-        x_sc = gather("x_sc", x_rows, offs_list, U8, 0, S)
-        wt_q = [quantise("wt0", wt_bf[0])]
-        acc_t = [psum.tile([P, G], F32, name="acc_t%d" % t) for t in range(TILES)]
-        for o in range(PASSES):
-            if o == 1:
-                shared = round_and_group("wt1", wt_raw[1], (nc.scalar.copy, nc.vector.tensor_copy))
-                wt_q.append(quantise("wt1", shared))
+        grouped, wt_q0 = weight_tiles("wt0")
+        for cols in halves:
+            round_and_group(nc.scalar.copy, grouped, wt_raw[0], cols)
+        quantise(wt_q0, grouped, whole)
+        e0 = gather("e0", e_tab[0], tch_list, U32)
+        for j in range(TILES):
+            teacher_pass(0, j, wt_q0, e0)
+        e1 = gather("e1", e_tab[1], tch_list, U32)
+        grouped, wt_q1 = weight_tiles("wt1")
+        for j in range(TILES):
+            round_and_group(nc.vector.tensor_copy if j % 2 == 0 else nc.scalar.copy, grouped, wt_raw[1], blocks[j])
+            quantise(wt_q1, grouped, blocks[j])
+            teacher_pass(1, j, wt_q1, e1)
+        for j in range(TILES):
+            turned = keep.tile([P, S], F32, name="turned%d" % j)
+            nc.scalar.activation(
+                turned[:], acc_t[j][:], ACT.Identity, bias=cen_col[:, j : j + 1], scale=-TEACHER_GAIN
+            )
             for t in range(TILES):
-                if t % 2 == 0:
-                    picked = gather("e%d_%d" % (o, t), e_tab[o], tch_list, U32, t * P, 2 * P)
-                mx_pass(acc_t[t], o, picked, slice((t % 2) * P, (t % 2 + 1) * P), e_sc, t, wt_q[o])
+                nc.tensor.transpose(neg_z[t][:, blocks[j]], turned[:, blocks[t]], ident[:])
 
-        acc_s = [psum.tile([P, G], F32, name="acc_s%d" % t) for t in range(TILES)]
-        ws_q = [quantise("ws0", ws_bf[0])]
-        for t in range(TILES):
-            if t % 2 == 0:
-                x0 = gather("x0_%d" % t, x_tab[0], offs_list, U32, t * P, 2 * P)
-            mx_pass(acc_s[t], 0, x0, slice((t % 2) * P, (t % 2 + 1) * P), x_sc, t, ws_q[0])
-        ws_q.append(quantise("ws1", ws_bf[1]))
-        for t in range(TILES):
-            x1 = gather("x1_%d" % t, x_tab[1], offs_list, U32, t * P, P)
-            mx_pass(acc_s[t], 1, x1, slice(0, P), x_sc, t, ws_q[1])
+        x_picked = [gather("x%d" % o, x_tab[o], offs_list, U32) for o in range(PASSES)]
+        grouped, ws_q0 = weight_tiles("ws0")
+        for cols in halves:
+            round_and_group(nc.scalar.copy, grouped, ws_raw[0], cols)
+        quantise(ws_q0, grouped, whole)
+        grouped, ws_q1 = weight_tiles("ws1")
+        round_and_group(nc.scalar.copy, grouped, ws_raw[1], halves[0])
+        round_and_group(nc.vector.tensor_copy, grouped, ws_raw[1], halves[1])
+        quantise(ws_q1, grouped, whole)
+        acc_s = []
 
-        t_exp = [ws_raw[t // 2][:, t % 2, :] for t in range(TILES)]
-        t_inv = []
+        def student_tile(t, bank):
+            acc = psum.tile([P, G], F32, name="acc_s%d" % t, tag=bank)
+            for o, weight in enumerate((ws_q0, ws_q1)):
+                nc.tensor.matmul_mx(
+                    out=acc[:],
+                    lhsT=x_picked[o][:, blocks[t]].bitcast(FP8X4),
+                    lhsT_scale=x_sc[SCALE_ROWS * o :, blocks[t]],
+                    rhs=weight[0][:].bitcast(FP8X4),
+                    rhs_scale=weight[1][:],
+                    start=(o == 0),
+                    stop=(o == PASSES - 1),
+                )
+            acc_s.append(acc)
+
+        student_tile(0, "acc0")
+        student_tile(1, "acc1")
+
+        t_exp = ws_raw[1]
+        prob = []
         for pair in range(TILES // 2):
-            neg = keep.tile([P, 2, G], F32, name="t_neg%d" % pair)
-            for u in range(2):
-                nc.vector.tensor_tensor(neg[:, u, :], cen_sb[:], acc_t[2 * pair + u][:], ALU.subtract)
-            low = keep.tile([P, 2], F32, name="t_low%d" % pair)
-            nc.vector.tensor_reduce(low[:], neg[:], AX.X, ALU.min)
-            shift = keep.tile([P, 2], F32, name="t_shift%d" % pair)
-            t_sum = keep.tile([P, 2], F32, name="t_sum%d" % pair)
-            nc.scalar.mul(shift[:], low[:], 2.5)
+            total = keep.tile([P, 2], F32, name="t_sum%d" % pair)
             for u in range(2):
                 t = 2 * pair + u
+                low = keep.tile([P, 1], F32, name="t_low%d" % t)
+                nc.vector.tensor_reduce(low[:], neg_z[t][:], AX.X, ALU.min)
                 nc.scalar.activation(
-                    t_exp[t], neg[:, u, :], ACT.Exp, bias=shift[:, u : u + 1], scale=-2.5, accum_out=t_sum[:, u : u + 1]
+                    t_exp[:, t, :], neg_z[t][:], ACT.Exp, bias=low[:], scale=-1.0, accum_out=total[:, u : u + 1]
                 )
             inv = keep.tile([P, 2], F32, name="t_inv%d" % pair)
-            nc.vector.reciprocal(inv[:], t_sum[:])
-            t_inv.extend([inv[:, 0:1], inv[:, 1:2]])
+            nc.vector.reciprocal(inv[:], total[:])
+            for u in range(2):
+                t = 2 * pair + u
+                p_t = keep.tile([P, G], F32, name="prob%d" % t)
+                nc.gpsimd.tensor_scalar(p_t[:], t_exp[:, t, :], inv[:, u : u + 1], 0.0, ALU.mult, ALU.add)
+                prob.append(p_t)
+
+        student_tile(2, "neg_z0")
+        student_tile(3, "neg_z1")
 
         s_exp = []
         s_sum = []
@@ -174,18 +219,21 @@ def tile_picked_ydino_grad_p_kernel(
             top = keep.tile([P, 1], F32, name="s_top%d" % t)
             nc.vector.tensor_reduce(top[:], acc_s[t][:], AX.X, ALU.max)
             shift = keep.tile([P, 1], F32, name="s_shift%d" % t)
-            nc.scalar.mul(shift[:], top[:], -1.5)
+            nc.scalar.mul(shift[:], top[:], -STUDENT_GAIN)
             ex = keep.tile([P, G], F32, name="s_exp%d" % t)
             total = keep.tile([P, 1], F32, name="s_sum%d" % t)
-            nc.scalar.activation(ex[:], acc_s[t][:], ACT.Exp, bias=shift[:], scale=1.5, accum_out=total[:])
+            nc.scalar.activation(
+                ex[:], acc_s[t][:], ACT.Exp, bias=shift[:], scale=STUDENT_GAIN, accum_out=total[:]
+            )
             s_exp.append(ex)
             s_sum.append(total)
 
         for t in range(TILES):
-            p_t = keep.tile([P, G], F32, name="prob%d" % t)
-            nc.scalar.activation(p_t[:], t_exp[t], ACT.Copy, scale=t_inv[t])
             inv = keep.tile([P, 1], F32, name="s_inv%d" % t)
             nc.vector.reciprocal(inv[:], s_sum[t][:])
             res = keep.tile([P, G], F32, name="res%d" % t)
-            nc.vector.scalar_tensor_tensor(res[:], s_exp[t][:], inv[:], p_t[:], ALU.mult, ALU.subtract)
-            nc.sync.dma_start(out[t * P : (t + 1) * P, :], res[:])
+            for cols in halves if t == TILES - 1 else [whole]:
+                nc.vector.scalar_tensor_tensor(
+                    res[:, cols], s_exp[t][:, cols], inv[:], prob[t][:, cols], ALU.mult, ALU.subtract
+                )
+                nc.sync.dma_start(out[blocks[t], cols], res[:, cols])

@@ -1,7 +1,6 @@
 from contextlib import ExitStack
 
 import concourse.mybir as mybir
-from concourse.masks import make_identity
 
 K = 1024
 T = 1024
@@ -30,10 +29,8 @@ PASSES = K // K_PASS
 TILES = S // P
 QUADRANTS = 4
 SCALE_ROWS = 4
-LIST_COLS = S // 16
+PER_COL = 16
 LINE = 4
-
-assert S == G
 
 
 def tile_picked_ydino_grad_p_kernel(
@@ -42,14 +39,14 @@ def tile_picked_ydino_grad_p_kernel(
     nc = tc.nc
     whole = slice(0, G)
     halves = [slice(0, G // 2), slice(G // 2, G)]
-    blocks = [slice(j * P, (j + 1) * P) for j in range(TILES)]
+    blocks = [slice(t * P, (t + 1) * P) for t in range(TILES)]
 
     with ExitStack() as ctx:
         keep = ctx.enter_context(tc.tile_pool(name="keep", bufs=1))
         psum = ctx.enter_context(tc.psum_pool(name="psum", bufs=1))
 
         def load_list(name, src):
-            tile = keep.tile([P, LIST_COLS], U16, name=name)
+            tile = keep.tile([P, S // PER_COL], U16, name=name)
             nc.sync.dma_start(tile[:], src)
             return tile
 
@@ -93,10 +90,32 @@ def tile_picked_ydino_grad_p_kernel(
                 in_=grouped[:, cols, :].rearrange("p c j -> p (c j)"),
             )
 
-        def gather(name, table, entries, dtype):
-            tile = keep.tile([P, S], dtype, name=name, align_bytes=64)
-            nc.vector.tensor_copy(tile[:], table[:].indirect(entries[:]))
+        def gather(name, table, entries, dtype, first, count):
+            tile = keep.tile([P, count], dtype, name=name, align_bytes=64)
+            offsets = entries[:, first // PER_COL : (first + count) // PER_COL]
+            nc.vector.tensor_copy(tile[:], table[:].indirect(offsets))
             return tile
+
+        def product_pass(name, acc, o, table, entries, picked_scales, weight):
+            for t in range(TILES):
+                if t % 2 == 0:
+                    picked = gather("%s%d_%d" % (name, o, t), table, entries, U32, t * P, 2 * P)
+                nc.tensor.matmul_mx(
+                    out=acc[t][:],
+                    lhsT=picked[:, blocks[t % 2]].bitcast(FP8X4),
+                    lhsT_scale=picked_scales[SCALE_ROWS * o :, blocks[t]],
+                    rhs=weight[0][:].bitcast(FP8X4),
+                    rhs_scale=weight[1][:],
+                    start=(o == 0),
+                    stop=(o == PASSES - 1),
+                )
+
+        def prepare(name, raw, second_copy):
+            grouped, weight = weight_tiles(name)
+            round_and_group(nc.scalar.copy, grouped, raw, halves[0])
+            round_and_group(second_copy, grouped, raw, halves[1])
+            quantise(weight, grouped, whole)
+            return weight
 
         x_rows = keep.tile([P, T], U8, name="x_rows", align_bytes=64)
         nc.gpsimd.memset(x_rows[:].bitcast(I32), 0)
@@ -106,112 +125,54 @@ def tile_picked_ydino_grad_p_kernel(
         wt_raw = [load_weight("wt_raw0", wt, 0)]
         load_scale_rows(x_rows, x_scales)
         offs_list = load_list("offs_list", offs)
-        cen_rows = keep.tile([P, P], F32, name="cen_rows")
-        nc.gpsimd.memset(cen_rows[:], 0.0)
-        nc.sync.dma_start(cen_rows[0:TILES, :], cen[0].rearrange("(j p) -> j p", p=P))
-        e_tab = [load_words("e_tab%d" % o, e_words, o, W) for o in range(PASSES)]
+        e_tab = [load_words("e_tab0", e_words, 0, W)]
         wt_raw.append(load_weight("wt_raw1", wt, 1))
-        x_tab = [load_words("x_tab%d" % o, x_words, o, T) for o in range(PASSES)]
+        e_tab.append(load_words("e_tab1", e_words, 1, W))
+        cen_sb = keep.tile([P, G], F32, name="cen_sb")
+        nc.sync.dma_start(cen_sb[:], cen)
         ws_raw = [load_weight("ws_raw%d" % o, ws, o) for o in range(PASSES)]
-
-        ident = keep.tile([P, P], F32, name="ident")
-        make_identity(nc, ident[:])
-
-        neg_z = [psum.tile([P, G], F32, name="neg_z%d" % t, tag="neg_z%d" % t) for t in range(TILES)]
-        nc.tensor.transpose(neg_z[0][:, 0:P], cen_rows[:], ident[:])
-        cen_col = keep.tile([P, TILES], F32, name="cen_col")
-        nc.scalar.mul(cen_col[:], neg_z[0][:, 0:TILES], TEACHER_GAIN)
+        x_tab = [load_words("x_tab%d" % o, x_words, o, T) for o in range(PASSES)]
 
         e_rows = keep.tile([P, W], U8, name="e_rows", align_bytes=64)
         nc.gpsimd.memset(e_rows[:].bitcast(I32), 0)
         for q in range(QUADRANTS):
             nc.vector.tensor_copy(e_rows[live_rows(q), :].bitcast(I32), e_stage[live_rows(q), :].bitcast(I32))
-        e_sc = gather("e_sc", e_rows, tch_list, U8)
-        x_sc = gather("x_sc", x_rows, offs_list, U8)
+        e_sc = gather("e_sc", e_rows, tch_list, U8, 0, S)
+        x_sc = gather("x_sc", x_rows, offs_list, U8, 0, S)
 
-        acc_t = [psum.tile([P, S], F32, name="acc_t%d" % j, tag="acc%d" % j) for j in range(TILES)]
+        acc_t = [psum.tile([P, G], F32, name="acc_t%d" % t) for t in range(TILES)]
+        acc_s = [psum.tile([P, G], F32, name="acc_s%d" % t) for t in range(TILES)]
+        for o, second_copy in enumerate((nc.scalar.copy, nc.vector.tensor_copy)):
+            weight = prepare("wt%d" % o, wt_raw[o], second_copy)
+            product_pass("e", acc_t, o, e_tab[o], tch_list, e_sc, weight)
+        for o in range(PASSES):
+            weight = prepare("ws%d" % o, ws_raw[o], nc.scalar.copy)
+            product_pass("x", acc_s, o, x_tab[o], offs_list, x_sc, weight)
 
-        def teacher_pass(o, j, weight, picked):
-            nc.tensor.matmul_mx(
-                out=acc_t[j][:],
-                lhsT=weight[0][:, blocks[j]].bitcast(FP8X4),
-                lhsT_scale=weight[1][:, blocks[j]],
-                rhs=picked[:].bitcast(FP8X4),
-                rhs_scale=e_sc[SCALE_ROWS * o :, :],
-                start=(o == 0),
-                stop=(o == PASSES - 1),
-            )
-
-        grouped, wt_q0 = weight_tiles("wt0")
-        for cols in halves:
-            round_and_group(nc.scalar.copy, grouped, wt_raw[0], cols)
-        quantise(wt_q0, grouped, whole)
-        e0 = gather("e0", e_tab[0], tch_list, U32)
-        for j in range(TILES):
-            teacher_pass(0, j, wt_q0, e0)
-        e1 = gather("e1", e_tab[1], tch_list, U32)
-        grouped, wt_q1 = weight_tiles("wt1")
-        for j in range(TILES):
-            round_and_group(nc.vector.tensor_copy if j % 2 == 0 else nc.scalar.copy, grouped, wt_raw[1], blocks[j])
-            quantise(wt_q1, grouped, blocks[j])
-            teacher_pass(1, j, wt_q1, e1)
-        for j in range(TILES):
-            turned = keep.tile([P, S], F32, name="turned%d" % j)
-            nc.scalar.activation(
-                turned[:], acc_t[j][:], ACT.Identity, bias=cen_col[:, j : j + 1], scale=-TEACHER_GAIN
-            )
-            for t in range(TILES):
-                nc.tensor.transpose(neg_z[t][:, blocks[j]], turned[:, blocks[t]], ident[:])
-
-        x_picked = [gather("x%d" % o, x_tab[o], offs_list, U32) for o in range(PASSES)]
-        grouped, ws_q0 = weight_tiles("ws0")
-        for cols in halves:
-            round_and_group(nc.scalar.copy, grouped, ws_raw[0], cols)
-        quantise(ws_q0, grouped, whole)
-        grouped, ws_q1 = weight_tiles("ws1")
-        round_and_group(nc.scalar.copy, grouped, ws_raw[1], halves[0])
-        round_and_group(nc.vector.tensor_copy, grouped, ws_raw[1], halves[1])
-        quantise(ws_q1, grouped, whole)
-        acc_s = []
-
-        def student_tile(t, bank):
-            acc = psum.tile([P, G], F32, name="acc_s%d" % t, tag=bank)
-            for o, weight in enumerate((ws_q0, ws_q1)):
-                nc.tensor.matmul_mx(
-                    out=acc[:],
-                    lhsT=x_picked[o][:, blocks[t]].bitcast(FP8X4),
-                    lhsT_scale=x_sc[SCALE_ROWS * o :, blocks[t]],
-                    rhs=weight[0][:].bitcast(FP8X4),
-                    rhs_scale=weight[1][:],
-                    start=(o == 0),
-                    stop=(o == PASSES - 1),
-                )
-            acc_s.append(acc)
-
-        student_tile(0, "acc0")
-        student_tile(1, "acc1")
-
-        t_exp = ws_raw[1]
-        prob = []
-        for pair in range(TILES // 2):
-            total = keep.tile([P, 2], F32, name="t_sum%d" % pair)
-            for u in range(2):
-                t = 2 * pair + u
+        diff = [keep.tile([P, G], F32, name="diff%d" % t) for t in range(TILES)]
+        t_exp = [ws_raw[t // 2][:, t % 2, :] for t in range(TILES)]
+        t_sum = [keep.tile([P, 2], F32, name="t_sum%d" % pair) for pair in range(TILES // 2)]
+        t_inv = [keep.tile([P, 2], F32, name="t_inv%d" % pair) for pair in range(TILES // 2)]
+        for step in range(TILES + 1):
+            if step < TILES:
+                nc.vector.tensor_tensor(diff[step][:], cen_sb[:], acc_t[step][:], ALU.subtract)
+            if step > 0:
+                t = step - 1
+                pair, u = divmod(t, 2)
                 low = keep.tile([P, 1], F32, name="t_low%d" % t)
-                nc.vector.tensor_reduce(low[:], neg_z[t][:], AX.X, ALU.min)
+                nc.vector.tensor_reduce(low[:], diff[t][:], AX.X, ALU.min)
+                shift = keep.tile([P, 1], F32, name="t_shift%d" % t)
+                nc.scalar.mul(shift[:], low[:], TEACHER_GAIN)
                 nc.scalar.activation(
-                    t_exp[:, t, :], neg_z[t][:], ACT.Exp, bias=low[:], scale=-1.0, accum_out=total[:, u : u + 1]
+                    t_exp[t],
+                    diff[t][:],
+                    ACT.Exp,
+                    bias=shift[:],
+                    scale=-TEACHER_GAIN,
+                    accum_out=t_sum[pair][:, u : u + 1],
                 )
-            inv = keep.tile([P, 2], F32, name="t_inv%d" % pair)
-            nc.vector.reciprocal(inv[:], total[:])
-            for u in range(2):
-                t = 2 * pair + u
-                p_t = keep.tile([P, G], F32, name="prob%d" % t)
-                nc.gpsimd.tensor_scalar(p_t[:], t_exp[:, t, :], inv[:, u : u + 1], 0.0, ALU.mult, ALU.add)
-                prob.append(p_t)
-
-        student_tile(2, "neg_z0")
-        student_tile(3, "neg_z1")
+                if u == 1:
+                    nc.vector.reciprocal(t_inv[pair][:], t_sum[pair][:])
 
         s_exp = []
         s_sum = []
@@ -228,12 +189,18 @@ def tile_picked_ydino_grad_p_kernel(
             s_exp.append(ex)
             s_sum.append(total)
 
-        for t in range(TILES):
-            inv = keep.tile([P, 1], F32, name="s_inv%d" % t)
-            nc.vector.reciprocal(inv[:], s_sum[t][:])
-            res = keep.tile([P, G], F32, name="res%d" % t)
-            for cols in halves if t == TILES - 1 else [whole]:
-                nc.vector.scalar_tensor_tensor(
-                    res[:, cols], s_exp[t][:, cols], inv[:], prob[t][:, cols], ALU.mult, ALU.subtract
-                )
-                nc.sync.dma_start(out[blocks[t], cols], res[:, cols])
+        prob = [keep.tile([P, G], F32, name="prob%d" % t) for t in range(TILES)]
+        s_inv = [keep.tile([P, 1], F32, name="s_inv%d" % t) for t in range(TILES)]
+        for step in range(TILES + 1):
+            if step < TILES:
+                pair, u = divmod(step, 2)
+                nc.scalar.activation(prob[step][:], t_exp[step], ACT.Copy, scale=t_inv[pair][:, u : u + 1])
+                nc.vector.reciprocal(s_inv[step][:], s_sum[step][:])
+            if step > 0:
+                t = step - 1
+                res = keep.tile([P, G], F32, name="res%d" % t)
+                for cols in halves if t == TILES - 1 else [whole]:
+                    nc.vector.scalar_tensor_tensor(
+                        res[:, cols], s_exp[t][:, cols], s_inv[t][:], prob[t][:, cols], ALU.mult, ALU.subtract
+                    )
+                    nc.sync.dma_start(out[blocks[t], cols], res[:, cols])

from contextlib import ExitStack

import concourse.mybir as mybir

K = 1024
T = 1024
W = 2048
S = 512
G = 512
STUDENT_GAIN = 1.5
TEACHER_GAIN = 2.5
FLOPS = 2 * 2 * K * S * G

F32 = mybir.dt.float32
BF16 = mybir.dt.bfloat16
I32 = mybir.dt.int32
U32 = mybir.dt.uint32
U16 = mybir.dt.uint16
U8 = mybir.dt.uint8
FP8X4 = mybir.dt.float8_e4m3fn_x4
ALU = mybir.AluOpType
ACT = mybir.ActivationFunctionType
AX = mybir.AxisListType

P = 128
PACK = 4
K_PASS = P * PACK
PASSES = K // K_PASS
TILES = S // P
QUADRANTS = 4
SCALE_ROWS = 4
PER_COL = 16
LINE = 4


def tile_picked_ydino_grad_p_kernel(
    tc, x_words, x_scales, e_words, e_scales, ws, wt, cen, offs, tch, out
):
    nc = tc.nc
    whole = slice(0, G)
    halves = [slice(0, G // 2), slice(G // 2, G)]
    blocks = [slice(t * P, (t + 1) * P) for t in range(TILES)]

    with ExitStack() as ctx:
        keep = ctx.enter_context(tc.tile_pool(name="keep", bufs=1))
        psum = ctx.enter_context(tc.psum_pool(name="psum", bufs=1))

        def load_list(name, src):
            tile = keep.tile([P, S // PER_COL], U16, name=name)
            nc.sync.dma_start(tile[:], src)
            return tile

        def live_rows(q):
            return slice(32 * q, 32 * q + SCALE_ROWS * PASSES)

        def load_scale_rows(tile, src):
            for q in range(QUADRANTS):
                nc.sync.dma_start(
                    tile[live_rows(q), :].bitcast(I32),
                    src[:, SCALE_ROWS * q : SCALE_ROWS * (q + 1), :].bitcast(I32),
                )

        def load_words(name, src, o, width):
            tile = keep.tile([P, width], U32, name=name, align_bytes=64)
            nc.sync.dma_start(tile[:].bitcast(I32), src[o].rearrange("p n t -> p (n t)").bitcast(I32))
            return tile

        def load_weight(name, src, o):
            tile = keep.tile([P, PACK, G], F32, name=name)
            rows = src[o * K_PASS : (o + 1) * K_PASS, :]
            nc.sync.dma_start(tile[:], rows.rearrange("(p j) g -> p j g", j=PACK))
            return tile

        def weight_tiles(name):
            grouped = keep.tile([P, G, PACK], BF16, name=name + "_bf", align_bytes=64)
            codes = keep.tile([P, G], U32, name=name + "_codes", align_bytes=64)
            scales = keep.tile([P, G], U8, name=name + "_scales", align_bytes=64)
            return grouped, (codes, scales)

        def round_and_group(copy, grouped, raw, cols):
            copy(
                grouped[:, cols, :].rearrange("p (c i) j -> p c j i", i=LINE),
                raw[:, :, cols].rearrange("p j (c i) -> p c j i", i=LINE),
            )

        def quantise(weight, grouped, cols):
            nc.vector.quantize_mx(
                out=weight[0][:, cols].bitcast(FP8X4),
                scales=weight[1][:, cols],
                in_=grouped[:, cols, :].rearrange("p c j -> p (c j)"),
            )

        def gather(name, table, entries, dtype, first, count):
            tile = keep.tile([P, count], dtype, name=name, align_bytes=64)
            offsets = entries[:, first // PER_COL : (first + count) // PER_COL]
            nc.vector.tensor_copy(tile[:], table[:].indirect(offsets))
            return tile

        def product_pass(name, acc, o, table, entries, picked_scales, weight):
            for t in range(TILES):
                if t % 2 == 0:
                    picked = gather("%s%d_%d" % (name, o, t), table, entries, U32, t * P, 2 * P)
                nc.tensor.matmul_mx(
                    out=acc[t][:],
                    lhsT=picked[:, blocks[t % 2]].bitcast(FP8X4),
                    lhsT_scale=picked_scales[SCALE_ROWS * o :, blocks[t]],
                    rhs=weight[0][:].bitcast(FP8X4),
                    rhs_scale=weight[1][:],
                    start=(o == 0),
                    stop=(o == PASSES - 1),
                )

        def prepare(name, raw, second_copy):
            grouped, weight = weight_tiles(name)
            round_and_group(nc.scalar.copy, grouped, raw, halves[0])
            round_and_group(second_copy, grouped, raw, halves[1])
            quantise(weight, grouped, whole)
            return weight

        x_rows = keep.tile([P, T], U8, name="x_rows", align_bytes=64)
        nc.gpsimd.memset(x_rows[:].bitcast(I32), 0)
        e_stage = keep.tile([P, W], U8, name="e_stage", align_bytes=64)
        tch_list = load_list("tch_list", tch)
        load_scale_rows(e_stage, e_scales)
        wt_raw = [load_weight("wt_raw0", wt, 0)]
        load_scale_rows(x_rows, x_scales)
        offs_list = load_list("offs_list", offs)
        e_tab = [load_words("e_tab0", e_words, 0, W)]
        wt_raw.append(load_weight("wt_raw1", wt, 1))
        e_tab.append(load_words("e_tab1", e_words, 1, W))
        cen_sb = keep.tile([P, G], F32, name="cen_sb")
        nc.sync.dma_start(cen_sb[:], cen)
        ws_raw = [load_weight("ws_raw%d" % o, ws, o) for o in range(PASSES)]
        x_tab = [load_words("x_tab%d" % o, x_words, o, T) for o in range(PASSES)]

        e_rows = keep.tile([P, W], U8, name="e_rows", align_bytes=64)
        nc.gpsimd.memset(e_rows[:].bitcast(I32), 0)
        for q in range(QUADRANTS):
            nc.vector.tensor_copy(e_rows[live_rows(q), :].bitcast(I32), e_stage[live_rows(q), :].bitcast(I32))
        e_sc = gather("e_sc", e_rows, tch_list, U8, 0, S)
        x_sc = gather("x_sc", x_rows, offs_list, U8, 0, S)

        acc_t = [psum.tile([P, G], F32, name="acc_t%d" % t) for t in range(TILES)]
        acc_s = [psum.tile([P, G], F32, name="acc_s%d" % t) for t in range(TILES)]
        for o, second_copy in enumerate((nc.scalar.copy, nc.vector.tensor_copy)):
            weight = prepare("wt%d" % o, wt_raw[o], second_copy)
            product_pass("e", acc_t, o, e_tab[o], tch_list, e_sc, weight)
        for o in range(PASSES):
            weight = prepare("ws%d" % o, ws_raw[o], nc.scalar.copy)
            product_pass("x", acc_s, o, x_tab[o], offs_list, x_sc, weight)

        diff = [keep.tile([P, G], F32, name="diff%d" % t) for t in range(TILES)]
        t_exp = [ws_raw[t // 2][:, t % 2, :] for t in range(TILES)]
        t_sum = [keep.tile([P, 2], F32, name="t_sum%d" % pair) for pair in range(TILES // 2)]
        t_inv = [keep.tile([P, 2], F32, name="t_inv%d" % pair) for pair in range(TILES // 2)]
        for step in range(TILES + 1):
            if step < TILES:
                nc.vector.tensor_tensor(diff[step][:], cen_sb[:], acc_t[step][:], ALU.subtract)
            if step > 0:
                t = step - 1
                pair, u = divmod(t, 2)
                low = keep.tile([P, 1], F32, name="t_low%d" % t)
                nc.vector.tensor_reduce(low[:], diff[t][:], AX.X, ALU.min)
                shift = keep.tile([P, 1], F32, name="t_shift%d" % t)
                nc.scalar.mul(shift[:], low[:], TEACHER_GAIN)
                nc.scalar.activation(
                    t_exp[t],
                    diff[t][:],
                    ACT.Exp,
                    bias=shift[:],
                    scale=-TEACHER_GAIN,
                    accum_out=t_sum[pair][:, u : u + 1],
                )
                if u == 1:
                    nc.vector.reciprocal(t_inv[pair][:], t_sum[pair][:])

        s_exp = []
        s_sum = []
        for t in range(TILES):
            top = keep.tile([P, 1], F32, name="s_top%d" % t)
            nc.vector.tensor_reduce(top[:], acc_s[t][:], AX.X, ALU.max)
            shift = keep.tile([P, 1], F32, name="s_shift%d" % t)
            nc.scalar.mul(shift[:], top[:], -STUDENT_GAIN)
            ex = keep.tile([P, G], F32, name="s_exp%d" % t)
            total = keep.tile([P, 1], F32, name="s_sum%d" % t)
            nc.scalar.activation(
                ex[:], acc_s[t][:], ACT.Exp, bias=shift[:], scale=STUDENT_GAIN, accum_out=total[:]
            )
            s_exp.append(ex)
            s_sum.append(total)

        prob = [keep.tile([P, G], F32, name="prob%d" % t) for t in range(TILES)]
        s_inv = [keep.tile([P, 1], F32, name="s_inv%d" % t) for t in range(TILES)]
        for step in range(TILES + 1):
            if step < TILES:
                pair, u = divmod(step, 2)
                nc.scalar.activation(prob[step][:], t_exp[step], ACT.Copy, scale=t_inv[pair][:, u : u + 1])
                nc.vector.reciprocal(s_inv[step][:], s_sum[step][:])
            if step > 0:
                t = step - 1
                res = keep.tile([P, G], F32, name="res%d" % t)
                for cols in halves if t == TILES - 1 else [whole]:
                    nc.vector.scalar_tensor_tensor(
                        res[:, cols], s_exp[t][:, cols], s_inv[t][:], prob[t][:, cols], ALU.mult, ALU.subtract
                    )
                    nc.sync.dma_start(out[blocks[t], cols], res[:, cols])
